import numpy as np
import ml_dtypes


def mxq(x, axis, fmt="e4m3"):
    dtype, down = {"e4m3": (ml_dtypes.float8_e4m3fn, 7), "e5m2": (ml_dtypes.float8_e5m2, 14)}[fmt]
    v = np.moveaxis(np.asarray(x, np.float32).astype(ml_dtypes.bfloat16).astype(np.float64), axis, -1)
    blocks = v.reshape(v.shape[:-1] + (-1, 32))
    amax = np.abs(blocks).max(-1, keepdims=True)
    byte = np.maximum(np.where(amax > 0, np.frexp(amax)[1] - 1 + 127, 0) - down, 1)
    scale = np.exp2(byte - 127.0)
    codes = (blocks / scale).astype(np.float32).astype(dtype).astype(np.float64)
    return np.moveaxis((codes * scale).reshape(v.shape), -1, axis)


WIDE = False


def mx_kscale(k):
    if not WIDE:
        return np.ones(k)
    levels = np.array([10, -10, 5, -5, 0])
    if k % 512:
        return np.exp2(np.random.permutation(np.resize(levels, k // 32))).repeat(32)
    a = np.empty((k // 512, 16))
    for p in range(k // 512):
        a[p, :8] = np.random.permutation(np.resize(levels, 8))
        for g in range(8):
            far = levels[np.abs(levels - a[p, g]) >= 10]
            a[p, g + 8] = far[np.random.randint(len(far))]
    return np.exp2(a.ravel()).repeat(32)


def f64(x):
    return np.asarray(x).astype(np.float64)


def striped(idx):
    return np.tile(np.asarray(idx).reshape(-1, 16).T, (8, 1)).astype(np.uint16)


def unstriped(offs):
    return offs[:16].T.reshape(-1).astype(np.int64)


E2M1 = np.array([0.0, 0.5, 1.0, 1.5, 2.0, 3.0, 4.0, 6.0, -0.0, -0.5, -1.0, -1.5, -2.0, -3.0, -4.0, -6.0])


def pack_weight(w, fmt):
    k, n = w.shape
    w = f64(np.asarray(w, np.float32).astype(ml_dtypes.bfloat16)).reshape(k // 32, 32, n)
    amax = np.abs(w).max(1)
    if fmt == "e4m3":
        byte = np.frexp(amax)[1] - 1 + 127 - 7
    else:
        mant, ex = np.frexp(amax / 6.0)
        byte = np.where(mant > 0.5, ex, ex - 1) + 127
    byte = np.clip(np.where(amax > 0, byte, 1), 1, 254)
    scaled = (w * np.exp2(127.0 - byte)[:, None, :]).reshape(k, n).astype(np.float32)
    by_word = np.ascontiguousarray(scaled.reshape(k // 512, 128, 4, n).transpose(0, 1, 3, 2))
    if fmt == "e4m3":
        words = by_word.astype(ml_dtypes.float8_e4m3fn).view(np.uint8)
    else:
        c = by_word.astype(ml_dtypes.float4_e2m1fn).view(np.uint8) & 0xF
        words = (c[..., 0::2] | (c[..., 1::2] << 4)).reshape(k // 512, 128, 2 * n)
    return np.ascontiguousarray(words), np.ascontiguousarray(byte.astype(np.uint8).reshape(k // 512, 16, n))


def unpack_weight(words, scales, fmt):
    g, _, n = scales.shape
    words = np.ascontiguousarray(words).reshape(g, 128, n, -1)
    if fmt == "e4m3":
        vals = words.view(ml_dtypes.float8_e4m3fn).astype(np.float64)
    else:
        nib = np.empty((g, 128, n, 4), np.uint8)
        nib[..., 0::2] = words & 0xF
        nib[..., 1::2] = words >> 4
        vals = E2M1[nib]
    vals = vals * np.repeat(np.exp2(scales.astype(np.float64) - 127.0), 8, axis=1)[..., None]
    return vals.transpose(0, 1, 3, 2).reshape(g * 512, n)


def bf(x):
    return np.asarray(x, np.float32).astype(ml_dtypes.bfloat16)


def planes(Y):
    r, m = Y.shape
    b = f64(bf(Y)).reshape(r // 32, 32, m)
    amax = np.abs(b).max(1)
    byte = np.clip(np.where(amax > 0, np.frexp(amax)[1] - 1 + 127 - 7, 1), 1, 254)
    codes = (b * np.exp2(127.0 - byte)[:, None, :]).reshape(r, m).astype(np.float32).astype(ml_dtypes.float8_e4m3fn).view(np.uint8)
    words = codes.reshape(r // 512, 128, 4, m).transpose(0, 1, 3, 2)
    return np.ascontiguousarray(words), np.ascontiguousarray(byte.astype(np.uint8).reshape(r // 512, 16, m))


B, N, T, D, NQ = 1, 512, 2048, 512, 512


def setup_inputs():
    n = np.random.standard_normal
    seg = T // B
    idx = np.concatenate([b * seg + np.random.permutation(seg)[:N] for b in range(B)])
    s = mx_kscale(D)[:, None]
    kp = pack_weight(n((D, T)) / s, "e4m3")
    return {
        "qT": (n((B, D, NQ)) * s * (0.50 / np.sqrt(D))).astype(np.float32),
        "k_words": kp[0],
        "k_scales": kp[1],
        "offs": striped(idx),
    }


def reference(qT, k_words, k_scales, offs):
    idx = unstriped(offs)
    pick = lambda x, which: x[:, which].reshape(x.shape[0], B, -1).transpose(1, 0, 2)
    k = unpack_weight(k_words, k_scales, "e4m3")
    kg = pick(k, idx)
    qq = mxq(f64(qT), 1, "e4m3")
    a = kg.transpose(0, 2, 1) @ qq
    y = np.square(a + 1.0)
    Y = y[0]
    words, scales = planes(Y)
    return Y, words, scales

@@ -1,0 +1,123 @@
+from contextlib import ExitStack
+
+import concourse.mybir as mybir
+
+F32 = mybir.dt.float32
+BF16 = mybir.dt.bfloat16
+I32 = mybir.dt.int32
+U32 = mybir.dt.uint32
+U16 = mybir.dt.uint16
+U8 = mybir.dt.uint8
+FP8X4 = mybir.dt.float8_e4m3fn_x4
+SQUARE = mybir.ActivationFunctionType.Square
+
+P = 128
+PACK = 4
+SLOTS, TOKENS, D, NQ = 512, 2048, 512, 512
+QLOAD = 256
+QC = 128
+FLOPS = 2 * SLOTS * D * NQ
+
+
+def interleave(copy, dst, src):
+    copy(dst.rearrange("p (c i) t -> p c t i", i=4), src.rearrange("p t (c i) -> p c t i", i=4))
+
+
+def tile_attend_plw_poly_seg_kernel(tc, qT, k_words, k_scales, offs, out_0, out_1, out_2):
+    nc = tc.nc
+    with ExitStack() as ctx:
+        sb = ctx.enter_context(tc.tile_pool(name="sb", bufs=1))
+        psum = ctx.enter_context(tc.psum_pool(name="psum", bufs=1))
+
+        offsets = sb.tile([P, SLOTS // 16], U16, name="offsets")
+        pool_scales = sb.tile([P, TOKENS], U8, name="pool_scales", align_bytes=64)
+        pool_words = sb.tile([P, TOKENS], I32, name="pool_words", align_bytes=64)
+        nc.vector.memset(pool_scales[:].bitcast(I32), 0)
+        nc.sync.dma_start(offsets[:], offs)
+        for quad in range(4):
+            nc.scalar.dma_start(
+                pool_scales[32 * quad : 32 * quad + 4, :].bitcast(I32),
+                k_scales[0, 4 * quad : 4 * quad + 4, :].bitcast(I32),
+            )
+        nc.sync.dma_start(pool_words[:], k_words[0].rearrange("p t r -> p (t r)").bitcast(I32))
+        q_rows = qT[0].rearrange("(p t) q -> p t q", t=PACK)
+        q_raw = []
+        for h in range(NQ // QLOAD):
+            raw = sb.tile([P, PACK, QLOAD], F32, name="q_raw%d" % h)
+            nc.sync.dma_start(raw[:], q_rows[:, :, h * QLOAD : (h + 1) * QLOAD])
+            q_raw.append(raw)
+
+        listed_scales = sb.tile([P, SLOTS], U8, name="listed_scales", align_bytes=64)
+        key_scales = sb.tile([P, SLOTS], U8, name="key_scales", align_bytes=64)
+        key_words = sb.tile([P, SLOTS], U32, name="key_words", align_bytes=64)
+        nc.vector.tensor_copy(listed_scales[:], pool_scales[:].indirect(offsets[:]))
+        nc.vector.tensor_copy(
+            key_scales[:].rearrange("p (u s) -> p u s", u=PACK),
+            listed_scales[:].rearrange("p (s u) -> p u s", u=PACK),
+        )
+        nc.vector.tensor_copy(
+            key_words[:].rearrange("p (u s) -> p s u", u=PACK),
+            pool_words[:].bitcast(U32).indirect(offsets[:]),
+        )
+
+        y_words = sb.tile([P, NQ], I32, name="y_words", align_bytes=64)
+        y_scales = sb.tile([P, NQ], U8, name="y_scales", align_bytes=64)
+        y_rows = out_0.rearrange("(p u) q -> p u q", u=PACK)
+        words_out = out_1[0].rearrange("p q u -> p (q u)").bitcast(I32)
+        chunks = NQ // QC
+        q_words, q_scales, q_bf, y = [], [], [], []
+
+        def round_queries(c):
+            grouped = sb.tile([P, QC, PACK], BF16, name="q_bf%d" % c, align_bytes=64)
+            first = (c * QC) % QLOAD
+            copy = nc.scalar.copy if c % 2 == 0 else nc.vector.tensor_copy
+            interleave(copy, grouped[:], q_raw[c * QC // QLOAD][:, :, first : first + QC])
+            q_bf.append(grouped)
+
+        def score(c):
+            words = sb.tile([P, QC], U32, name="q_words%d" % c, align_bytes=64)
+            scales = sb.tile([P, QC], U8, name="q_scales%d" % c, align_bytes=64)
+            nc.vector.quantize_mx(
+                out=words[:].bitcast(FP8X4), scales=scales[:], in_=q_bf[c][:].rearrange("p q t -> p (q t)")
+            )
+            bank = psum.tile([P, PACK, QC], F32, name="bank%d" % c)
+            for u in range(PACK):
+                nc.tensor.matmul_mx(
+                    out=bank[:, u, :],
+                    lhsT=key_words[:, u * P : (u + 1) * P].bitcast(FP8X4),
+                    lhsT_scale=key_scales[:, u * P : (u + 1) * P],
+                    rhs=words[:].bitcast(FP8X4),
+                    rhs_scale=scales[:],
+                    start=True,
+                    stop=True,
+                )
+            weights = sb.tile([P, PACK, QC], F32, name="y%d" % c)
+            nc.scalar.activation(weights[:], bank[:], SQUARE, bias=1.0)
+            nc.sync.dma_start(y_rows[:, :, c * QC : (c + 1) * QC], weights[:])
+            y.append(weights)
+
+        def hand_on(c):
+            cols = slice(c * QC, (c + 1) * QC)
+            grouped = sb.tile([P, QC, PACK], BF16, name="y_bf%d" % c, align_bytes=64)
+            interleave(nc.vector.tensor_copy, grouped[:], y[c][:])
+            nc.vector.quantize_mx(
+                out=y_words[:, cols].bitcast(FP8X4),
+                scales=y_scales[:, cols],
+                in_=grouped[:].rearrange("p q u -> p (q u)"),
+            )
+            if c % 2 == 1:
+                pair = slice((c - 1) * QC, (c + 1) * QC)
+                nc.sync.dma_start(words_out[:, pair], y_words[:, pair])
+
+        for c in range(chunks):
+            round_queries(c)
+        for c in range(chunks):
+            score(c)
+        for c in range(chunks):
+            hand_on(c)
+        for quad in range(4):
+            queue = nc.scalar if quad % 2 == 0 else nc.sync
+            queue.dma_start(
+                out_2[0, 4 * quad : 4 * quad + 4, :].bitcast(I32),
+                y_scales[32 * quad : 32 * quad + 4, :].bitcast(I32),
+            )

@@ -34,56 +34,67 @@ def tile_attend_plw_poly_seg_kernel(tc, qT, k_words, k_scales, offs, out_0, out_
         pool_words = sb.tile([P, TOKENS], I32, name="pool_words", align_bytes=64)
         nc.vector.memset(pool_scales[:].bitcast(I32), 0)
         nc.sync.dma_start(offsets[:], offs)
+        q_rows = qT[0].rearrange("(p t) q -> p t q", t=PACK)
+        q_raw = {}
+
+        def load_queries(first, last):
+            raw = sb.tile([P, PACK, (last - first) * QC], F32, name="q_raw%d" % first)
+            nc.sync.dma_start(raw[:], q_rows[:, :, first * QC : last * QC])
+            for c in range(first, last):
+                q_raw[c] = raw[:, :, (c - first) * QC : (c - first + 1) * QC]
+
+        load_queries(0, 1)
         for quad in range(4):
-            nc.scalar.dma_start(
+            nc.sync.dma_start(
                 pool_scales[32 * quad : 32 * quad + 4, :].bitcast(I32),
                 k_scales[0, 4 * quad : 4 * quad + 4, :].bitcast(I32),
             )
         nc.sync.dma_start(pool_words[:], k_words[0].rearrange("p t r -> p (t r)").bitcast(I32))
-        q_rows = qT[0].rearrange("(p t) q -> p t q", t=PACK)
-        q_raw = []
-        for h in range(NQ // QLOAD):
-            raw = sb.tile([P, PACK, QLOAD], F32, name="q_raw%d" % h)
-            nc.sync.dma_start(raw[:], q_rows[:, :, h * QLOAD : (h + 1) * QLOAD])
-            q_raw.append(raw)
+        load_queries(1, 2)
+        load_queries(2, 4)
 
         listed_scales = sb.tile([P, SLOTS], U8, name="listed_scales", align_bytes=64)
         key_scales = sb.tile([P, SLOTS], U8, name="key_scales", align_bytes=64)
         key_words = sb.tile([P, SLOTS], U32, name="key_words", align_bytes=64)
-        nc.vector.tensor_copy(listed_scales[:], pool_scales[:].indirect(offsets[:]))
-        nc.vector.tensor_copy(
-            key_scales[:].rearrange("p (u s) -> p u s", u=PACK),
-            listed_scales[:].rearrange("p (s u) -> p u s", u=PACK),
-        )
-        nc.vector.tensor_copy(
-            key_words[:].rearrange("p (u s) -> p s u", u=PACK),
-            pool_words[:].bitcast(U32).indirect(offsets[:]),
-        )
-
         y_words = sb.tile([P, NQ], I32, name="y_words", align_bytes=64)
         y_scales = sb.tile([P, NQ], U8, name="y_scales", align_bytes=64)
         y_rows = out_0.rearrange("(p u) q -> p u q", u=PACK)
         words_out = out_1[0].rearrange("p q u -> p (q u)").bitcast(I32)
-        chunks = NQ // QC
-        q_words, q_scales, q_bf, y = [], [], [], []
+        q_bf, q_mx, banks, y, y_bf = {}, {}, {}, {}, {}
 
-        def round_queries(c):
-            grouped = sb.tile([P, QC, PACK], BF16, name="q_bf%d" % c, align_bytes=64)
-            first = (c * QC) % QLOAD
-            copy = nc.scalar.copy if c % 2 == 0 else nc.vector.tensor_copy
-            interleave(copy, grouped[:], q_raw[c * QC // QLOAD][:, :, first : first + QC])
-            q_bf.append(grouped)
+        def gather_scales():
+            nc.vector.tensor_copy(listed_scales[:], pool_scales[:].indirect(offsets[:]))
 
-        def score(c):
+        def deal_scales():
+            nc.vector.tensor_copy(
+                key_scales[:].rearrange("p (u s) -> p u s", u=PACK),
+                listed_scales[:].rearrange("p (s u) -> p u s", u=PACK),
+            )
+
+        def gather_words():
+            nc.vector.tensor_copy(
+                key_words[:].rearrange("p (u s) -> p s u", u=PACK),
+                pool_words[:].bitcast(U32).indirect(offsets[:]),
+            )
+
+        def round_queries(c, copy):
+            q_bf[c] = sb.tile([P, QC, PACK], BF16, name="q_bf%d" % c, align_bytes=64)
+            interleave(copy, q_bf[c][:], q_raw[c])
+
+        def quantise_queries(c):
             words = sb.tile([P, QC], U32, name="q_words%d" % c, align_bytes=64)
             scales = sb.tile([P, QC], U8, name="q_scales%d" % c, align_bytes=64)
             nc.vector.quantize_mx(
                 out=words[:].bitcast(FP8X4), scales=scales[:], in_=q_bf[c][:].rearrange("p q t -> p (q t)")
             )
-            bank = psum.tile([P, PACK, QC], F32, name="bank%d" % c)
+            q_mx[c] = (words, scales)
+
+        def score(c):
+            words, scales = q_mx[c]
+            banks[c] = psum.tile([P, PACK, QC], F32, name="bank%d" % c)
             for u in range(PACK):
                 nc.tensor.matmul_mx(
-                    out=bank[:, u, :],
+                    out=banks[c][:, u, :],
                     lhsT=key_words[:, u * P : (u + 1) * P].bitcast(FP8X4),
                     lhsT_scale=key_scales[:, u * P : (u + 1) * P],
                     rhs=words[:].bitcast(FP8X4),
@@ -91,33 +102,69 @@ def tile_attend_plw_poly_seg_kernel(tc, qT, k_words, k_scales, offs, out_0, out_
                     start=True,
                     stop=True,
                 )
-            weights = sb.tile([P, PACK, QC], F32, name="y%d" % c)
-            nc.scalar.activation(weights[:], bank[:], SQUARE, bias=1.0)
-            nc.sync.dma_start(y_rows[:, :, c * QC : (c + 1) * QC], weights[:])
-            y.append(weights)
 
-        def hand_on(c):
+        def weigh(c):
+            y[c] = sb.tile([P, PACK, QC], F32, name="y%d" % c)
+            nc.scalar.activation(y[c][:], banks[c][:], SQUARE, bias=1.0)
+            nc.sync.dma_start(y_rows[:, :, c * QC : (c + 1) * QC], y[c][:])
+
+        def round_weights(c):
+            y_bf[c] = sb.tile([P, QC, PACK], BF16, name="y_bf%d" % c, align_bytes=64)
+            interleave(nc.vector.tensor_copy, y_bf[c][:], y[c][:])
+
+        def weigh_rounded(c):
+            y_bf[c] = sb.tile([P, QC, PACK], BF16, name="y_bf%d" % c, align_bytes=64)
+            nc.scalar.activation(y_bf[c][:], banks[c][:].rearrange("p u q -> p q u"), SQUARE, bias=1.0)
+
+        def quantise_weights(c):
             cols = slice(c * QC, (c + 1) * QC)
-            grouped = sb.tile([P, QC, PACK], BF16, name="y_bf%d" % c, align_bytes=64)
-            interleave(nc.vector.tensor_copy, grouped[:], y[c][:])
             nc.vector.quantize_mx(
                 out=y_words[:, cols].bitcast(FP8X4),
                 scales=y_scales[:, cols],
-                in_=grouped[:].rearrange("p q u -> p (q u)"),
+                in_=y_bf[c][:].rearrange("p q u -> p (q u)"),
             )
-            if c % 2 == 1:
-                pair = slice((c - 1) * QC, (c + 1) * QC)
-                nc.sync.dma_start(words_out[:, pair], y_words[:, pair])
 
-        for c in range(chunks):
-            round_queries(c)
-        for c in range(chunks):
-            score(c)
-        for c in range(chunks):
-            hand_on(c)
-        for quad in range(4):
-            queue = nc.scalar if quad % 2 == 0 else nc.sync
+        def store_words(first, last, queue):
+            cols = slice(first * QC, last * QC)
+            queue.dma_start(words_out[:, cols], y_words[:, cols])
+
+        def store_scales(quad, queue):
             queue.dma_start(
                 out_2[0, 4 * quad : 4 * quad + 4, :].bitcast(I32),
                 y_scales[32 * quad : 32 * quad + 4, :].bitcast(I32),
             )
+
+        on_scalar, on_vector = nc.scalar.copy, nc.vector.tensor_copy
+        gather_scales()
+        round_queries(0, on_scalar)
+        deal_scales()
+        quantise_queries(0)
+        gather_words()
+        round_queries(1, on_scalar)
+        score(0)
+        quantise_queries(1)
+        weigh(0)
+        round_queries(2, on_vector)
+        score(1)
+        round_queries(3, on_vector)
+        quantise_queries(2)
+        weigh(1)
+        score(2)
+        quantise_queries(3)
+        round_weights(0)
+        weigh(2)
+        score(3)
+        round_weights(1)
+        quantise_weights(0)
+        weigh(3)
+        quantise_weights(1)
+        round_weights(2)
+        round_weights(3)
+        quantise_weights(2)
+        store_words(0, 3, nc.sync)
+        quantise_weights(3)
+        store_words(3, 4, nc.scalar)
+        store_scales(0, nc.sync)
+        store_scales(1, nc.scalar)
+        store_scales(2, nc.sync)
+        store_scales(3, nc.scalar)

@@ -14,7 +14,7 @@ SQUARE = mybir.ActivationFunctionType.Square
 P = 128
 PACK = 4
 SLOTS, TOKENS, D, NQ = 512, 2048, 512, 512
-QLOAD = 256
+HEAD = 512
 QC = 128
 FLOPS = 2 * SLOTS * D * NQ
 
@@ -31,8 +31,10 @@ def tile_attend_plw_poly_seg_kernel(tc, qT, k_words, k_scales, offs, out_0, out_
 
         offsets = sb.tile([P, SLOTS // 16], U16, name="offsets")
         pool_scales = sb.tile([P, TOKENS], U8, name="pool_scales", align_bytes=64)
-        pool_words = sb.tile([P, TOKENS], I32, name="pool_words", align_bytes=64)
+        pool_words = sb.tile([P, TOKENS], I32, name="pool_words", tag="words0", align_bytes=64)
         nc.vector.memset(pool_scales[:].bitcast(I32), 0)
+        words_in = k_words[0].rearrange("p t r -> p (t r)").bitcast(I32)
+        nc.sync.dma_start(pool_words[:, :HEAD], words_in[:, :HEAD])
         nc.sync.dma_start(offsets[:], offs)
         q_rows = qT[0].rearrange("(p t) q -> p t q", t=PACK)
         q_raw = {}
@@ -43,15 +45,14 @@ def tile_attend_plw_poly_seg_kernel(tc, qT, k_words, k_scales, offs, out_0, out_
             for c in range(first, last):
                 q_raw[c] = raw[:, :, (c - first) * QC : (c - first + 1) * QC]
 
-        load_queries(0, 1)
-        for quad in range(4):
+        for quad in (0, 2, 1, 3):
             nc.sync.dma_start(
                 pool_scales[32 * quad : 32 * quad + 4, :].bitcast(I32),
                 k_scales[0, 4 * quad : 4 * quad + 4, :].bitcast(I32),
             )
-        nc.sync.dma_start(pool_words[:], k_words[0].rearrange("p t r -> p (t r)").bitcast(I32))
-        load_queries(1, 2)
-        load_queries(2, 4)
+        nc.sync.dma_start(pool_words[:, HEAD:], words_in[:, HEAD:])
+        for c in range(4):
+            load_queries(c, c + 1)
 
         listed_scales = sb.tile([P, SLOTS], U8, name="listed_scales", align_bytes=64)
         key_scales = sb.tile([P, SLOTS], U8, name="key_scales", align_bytes=64)
@@ -78,11 +79,11 @@ def tile_attend_plw_poly_seg_kernel(tc, qT, k_words, k_scales, offs, out_0, out_
             )
 
         def round_queries(c, copy):
-            q_bf[c] = sb.tile([P, QC, PACK], BF16, name="q_bf%d" % c, align_bytes=64)
+            q_bf[c] = sb.tile([P, QC, PACK], BF16, name="q_bf%d" % c, tag="q_bf%d" % (1 if c == 3 else c), align_bytes=64)
             interleave(copy, q_bf[c][:], q_raw[c])
 
         def quantise_queries(c):
-            words = sb.tile([P, QC], U32, name="q_words%d" % c, align_bytes=64)
+            words = sb.tile([P, QC], U32, name="q_words%d" % c, tag="words%d" % c, align_bytes=64)
             scales = sb.tile([P, QC], U8, name="q_scales%d" % c, align_bytes=64)
             nc.vector.quantize_mx(
                 out=words[:].bitcast(FP8X4), scales=scales[:], in_=q_bf[c][:].rearrange("p q t -> p (q t)")
@@ -136,34 +137,34 @@ def tile_attend_plw_poly_seg_kernel(tc, qT, k_words, k_scales, offs, out_0, out_
 
         on_scalar, on_vector = nc.scalar.copy, nc.vector.tensor_copy
         gather_scales()
-        round_queries(0, on_scalar)
         deal_scales()
-        quantise_queries(0)
         gather_words()
+        round_queries(0, on_scalar)
+        quantise_queries(0)
         round_queries(1, on_scalar)
         score(0)
         quantise_queries(1)
-        weigh(0)
-        round_queries(2, on_vector)
+        round_queries(2, on_scalar)
         score(1)
-        round_queries(3, on_vector)
+        weigh(0)
         quantise_queries(2)
-        weigh(1)
+        round_queries(3, on_vector)
         score(2)
-        quantise_queries(3)
+        weigh(1)
         round_weights(0)
-        weigh(2)
+        quantise_queries(3)
         score(3)
+        weigh(2)
         round_weights(1)
         quantise_weights(0)
-        weigh(3)
-        quantise_weights(1)
+        weigh_rounded(3)
         round_weights(2)
-        round_weights(3)
+        quantise_weights(1)
+        weigh(3)
+        store_words(0, 2, nc.sync)
         quantise_weights(2)
-        store_words(0, 3, nc.sync)
         quantise_weights(3)
-        store_words(3, 4, nc.scalar)
+        store_words(2, 4, nc.scalar)
         store_scales(0, nc.sync)
         store_scales(1, nc.scalar)
         store_scales(2, nc.sync)

@@ -30,8 +30,8 @@ def tile_attend_plw_poly_seg_kernel(tc, qT, k_words, k_scales, offs, out_0, out_
         psum = ctx.enter_context(tc.psum_pool(name="psum", bufs=1))
 
         offsets = sb.tile([P, SLOTS // 16], U16, name="offsets")
-        pool_scales = sb.tile([P, TOKENS], U8, name="pool_scales", align_bytes=64)
-        pool_words = sb.tile([P, TOKENS], I32, name="pool_words", tag="words0", align_bytes=64)
+        pool_scales = sb.tile([P, TOKENS], U8, name="pool_scales", align_bytes=256)
+        pool_words = sb.tile([P, TOKENS], I32, name="pool_words", tag="words0", align_bytes=256)
         nc.vector.memset(pool_scales[:].bitcast(I32), 0)
         words_in = k_words[0].rearrange("p t r -> p (t r)").bitcast(I32)
         nc.sync.dma_start(pool_words[:, :HEAD], words_in[:, :HEAD])
@@ -40,7 +40,7 @@ def tile_attend_plw_poly_seg_kernel(tc, qT, k_words, k_scales, offs, out_0, out_
         q_raw = {}
 
         def load_queries(first, last):
-            raw = sb.tile([P, PACK, (last - first) * QC], F32, name="q_raw%d" % first)
+            raw = sb.tile([P, PACK, (last - first) * QC], F32, name="q_raw%d" % first, align_bytes=256)
             nc.sync.dma_start(raw[:], q_rows[:, :, first * QC : last * QC])
             for c in range(first, last):
                 q_raw[c] = raw[:, :, (c - first) * QC : (c - first + 1) * QC]
@@ -57,8 +57,8 @@ def tile_attend_plw_poly_seg_kernel(tc, qT, k_words, k_scales, offs, out_0, out_
         listed_scales = sb.tile([P, SLOTS], U8, name="listed_scales", align_bytes=64)
         key_scales = sb.tile([P, SLOTS], U8, name="key_scales", align_bytes=64)
         key_words = sb.tile([P, SLOTS], U32, name="key_words", align_bytes=64)
-        y_words = sb.tile([P, NQ], I32, name="y_words", align_bytes=64)
-        y_scales = sb.tile([P, NQ], U8, name="y_scales", align_bytes=64)
+        y_words = sb.tile([P, NQ], I32, name="y_words", align_bytes=256)
+        y_scales = sb.tile([P, NQ], U8, name="y_scales", align_bytes=256)
         y_rows = out_0.rearrange("(p u) q -> p u q", u=PACK)
         words_out = out_1[0].rearrange("p q u -> p (q u)").bitcast(I32)
         q_bf, q_mx, banks, y, y_bf = {}, {}, {}, {}, {}
@@ -83,7 +83,7 @@ def tile_attend_plw_poly_seg_kernel(tc, qT, k_words, k_scales, offs, out_0, out_
             interleave(copy, q_bf[c][:], q_raw[c])
 
         def quantise_queries(c):
-            words = sb.tile([P, QC], U32, name="q_words%d" % c, tag="words%d" % c, align_bytes=64)
+            words = sb.tile([P, QC], U32, name="q_words%d" % c, tag="words%d" % c, align_bytes=256)
             scales = sb.tile([P, QC], U8, name="q_scales%d" % c, align_bytes=64)
             nc.vector.quantize_mx(
                 out=words[:].bitcast(FP8X4), scales=scales[:], in_=q_bf[c][:].rearrange("p q t -> p (q t)")
@@ -105,7 +105,7 @@ def tile_attend_plw_poly_seg_kernel(tc, qT, k_words, k_scales, offs, out_0, out_
                 )
 
         def weigh(c):
-            y[c] = sb.tile([P, PACK, QC], F32, name="y%d" % c)
+            y[c] = sb.tile([P, PACK, QC], F32, name="y%d" % c, align_bytes=256)
             nc.scalar.activation(y[c][:], banks[c][:], SQUARE, bias=1.0)
             nc.sync.dma_start(y_rows[:, :, c * QC : (c + 1) * QC], y[c][:])
 

@@ -14,7 +14,7 @@ SQUARE = mybir.ActivationFunctionType.Square
 P = 128
 PACK = 4
 SLOTS, TOKENS, D, NQ = 512, 2048, 512, 512
-HEAD = 512
+HEAD = 640
 QC = 128
 FLOPS = 2 * SLOTS * D * NQ
 
@@ -31,7 +31,7 @@ def tile_attend_plw_poly_seg_kernel(tc, qT, k_words, k_scales, offs, out_0, out_
 
         offsets = sb.tile([P, SLOTS // 16], U16, name="offsets")
         pool_scales = sb.tile([P, TOKENS], U8, name="pool_scales", align_bytes=256)
-        pool_words = sb.tile([P, TOKENS], I32, name="pool_words", tag="words0", align_bytes=256)
+        pool_words = sb.tile([P, TOKENS], I32, name="pool_words", align_bytes=256)
         nc.vector.memset(pool_scales[:].bitcast(I32), 0)
         words_in = k_words[0].rearrange("p t r -> p (t r)").bitcast(I32)
         nc.sync.dma_start(pool_words[:, :HEAD], words_in[:, :HEAD])

@@ -54,7 +54,6 @@ def tile_attend_plw_poly_seg_kernel(tc, qT, k_words, k_scales, offs, out_0, out_
         for c in range(4):
             load_queries(c, c + 1)
 
-        listed_scales = sb.tile([P, SLOTS], U8, name="listed_scales", align_bytes=64)
         key_scales = sb.tile([P, SLOTS], U8, name="key_scales", align_bytes=64)
         key_words = sb.tile([P, SLOTS], U32, name="key_words", align_bytes=64)
         y_words = sb.tile([P, NQ], I32, name="y_words", align_bytes=256)
@@ -64,12 +63,9 @@ def tile_attend_plw_poly_seg_kernel(tc, qT, k_words, k_scales, offs, out_0, out_
         q_bf, q_mx, banks, y, y_bf = {}, {}, {}, {}, {}
 
         def gather_scales():
-            nc.vector.tensor_copy(listed_scales[:], pool_scales[:].indirect(offsets[:]))
-
-        def deal_scales():
             nc.vector.tensor_copy(
-                key_scales[:].rearrange("p (u s) -> p u s", u=PACK),
-                listed_scales[:].rearrange("p (s u) -> p u s", u=PACK),
+                key_scales[:].rearrange("p (u s) -> p s u", u=PACK),
+                pool_scales[:].indirect(offsets[:]),
             )
 
         def gather_words():
@@ -137,7 +133,6 @@ def tile_attend_plw_poly_seg_kernel(tc, qT, k_words, k_scales, offs, out_0, out_
 
         on_scalar, on_vector = nc.scalar.copy, nc.vector.tensor_copy
         gather_scales()
-        deal_scales()
         gather_words()
         round_queries(0, on_scalar)
         quantise_queries(0)

@@ -14,7 +14,7 @@ SQUARE = mybir.ActivationFunctionType.Square
 P = 128
 PACK = 4
 SLOTS, TOKENS, D, NQ = 512, 2048, 512, 512
-HEAD = 640
+HEAD = 832
 QC = 128
 FLOPS = 2 * SLOTS * D * NQ
 

@@ -45,11 +45,8 @@ def tile_attend_plw_poly_seg_kernel(tc, qT, k_words, k_scales, offs, out_0, out_
             for c in range(first, last):
                 q_raw[c] = raw[:, :, (c - first) * QC : (c - first + 1) * QC]
 
-        for quad in (0, 2, 1, 3):
-            nc.sync.dma_start(
-                pool_scales[32 * quad : 32 * quad + 4, :].bitcast(I32),
-                k_scales[0, 4 * quad : 4 * quad + 4, :].bitcast(I32),
-            )
+        for r in range(4):
+            nc.sync.dma_start(pool_scales[r:P:32, :].bitcast(I32), k_scales[0, r:16:4, :].bitcast(I32))
         nc.sync.dma_start(pool_words[:, HEAD:], words_in[:, HEAD:])
         for c in range(4):
             load_queries(c, c + 1)

@@ -16,6 +16,7 @@ PACK = 4
 SLOTS, TOKENS, D, NQ = 512, 2048, 512, 512
 HEAD = 832
 QC = 128
+SHARED = 1
 FLOPS = 2 * SLOTS * D * NQ
 
 
@@ -86,9 +87,11 @@ def tile_attend_plw_poly_seg_kernel(tc, qT, k_words, k_scales, offs, out_0, out_
         def score(c):
             words, scales = q_mx[c]
             banks[c] = psum.tile([P, PACK, QC], F32, name="bank%d" % c)
+            if c == SHARED:
+                banks["side"] = psum.tile([P, QC], F32, name="side_bank")
             for u in range(PACK):
                 nc.tensor.matmul_mx(
-                    out=banks[c][:, u, :],
+                    out=banks["side"][:] if (c, u) == (SHARED, 0) else banks[c][:, u, :],
                     lhsT=key_words[:, u * P : (u + 1) * P].bitcast(FP8X4),
                     lhsT_scale=key_scales[:, u * P : (u + 1) * P],
                     rhs=words[:].bitcast(FP8X4),
@@ -100,6 +103,18 @@ def tile_attend_plw_poly_seg_kernel(tc, qT, k_words, k_scales, offs, out_0, out_
         def weigh(c):
             y[c] = sb.tile([P, PACK, QC], F32, name="y%d" % c, align_bytes=256)
             nc.scalar.activation(y[c][:], banks[c][:], SQUARE, bias=1.0)
+            nc.sync.dma_start(y_rows[:, :, c * QC : (c + 1) * QC], y[c][:])
+
+        def shift_on_vector():
+            y["shifted"] = sb.tile([P, QC], F32, name="shifted", tag="y_bf0", align_bytes=64)
+            nc.vector.tensor_scalar_add(y["shifted"][:], banks["side"][:], 1.0)
+
+        def weigh_shared(c):
+            y[c] = sb.tile([P, PACK, QC], F32, name="y%d" % c, align_bytes=256)
+            nc.scalar.activation(y[c][:, 1:, :], banks[c][:, 1:, :], SQUARE, bias=1.0)
+
+        def square_on_vector(c):
+            nc.vector.tensor_mul(y[c][:, 0, :], y["shifted"][:], y["shifted"][:])
             nc.sync.dma_start(y_rows[:, :, c * QC : (c + 1) * QC], y[c][:])
 
         def round_weights(c):
@@ -142,10 +157,12 @@ def tile_attend_plw_poly_seg_kernel(tc, qT, k_words, k_scales, offs, out_0, out_
         quantise_queries(2)
         round_queries(3, on_vector)
         score(2)
-        weigh(1)
-        round_weights(0)
+        weigh_shared(1)
+        shift_on_vector()
         quantise_queries(3)
         score(3)
+        square_on_vector(1)
+        round_weights(0)
         weigh(2)
         round_weights(1)
         quantise_weights(0)

@@ -76,6 +76,11 @@ def tile_attend_plw_poly_seg_kernel(tc, qT, k_words, k_scales, offs, out_0, out_
             q_bf[c] = sb.tile([P, QC, PACK], BF16, name="q_bf%d" % c, tag="q_bf%d" % (1 if c == 3 else c), align_bytes=64)
             interleave(copy, q_bf[c][:], q_raw[c])
 
+        def round_queries_in_halves(c):
+            q_bf[c] = sb.tile([P, QC, PACK], BF16, name="q_bf%d" % c, tag="q_bf0", align_bytes=64)
+            interleave(nc.scalar.copy, q_bf[c][:, : QC // 2, :], q_raw[c][:, :, : QC // 2])
+            interleave(nc.vector.tensor_copy, q_bf[c][:, QC // 2 :, :], q_raw[c][:, :, QC // 2 :])
+
         def quantise_queries(c):
             words = sb.tile([P, QC], U32, name="q_words%d" % c, tag="words%d" % c, align_bytes=256)
             scales = sb.tile([P, QC], U8, name="q_scales%d" % c, align_bytes=64)
@@ -151,7 +156,7 @@ def tile_attend_plw_poly_seg_kernel(tc, qT, k_words, k_scales, offs, out_0, out_
         round_queries(1, on_scalar)
         score(0)
         quantise_queries(1)
-        round_queries(2, on_scalar)
+        round_queries_in_halves(2)
         score(1)
         weigh(0)
         quantise_queries(2)

@@ -14,7 +14,7 @@ SQUARE = mybir.ActivationFunctionType.Square
 P = 128
 PACK = 4
 SLOTS, TOKENS, D, NQ = 512, 2048, 512, 512
-HEAD = 832
+HEAD = 768
 QC = 128
 SHARED = 1
 FLOPS = 2 * SLOTS * D * NQ
@@ -47,7 +47,8 @@ def tile_attend_plw_poly_seg_kernel(tc, qT, k_words, k_scales, offs, out_0, out_
                 q_raw[c] = raw[:, :, (c - first) * QC : (c - first + 1) * QC]
 
         for r in range(4):
-            nc.sync.dma_start(pool_scales[r:P:32, :].bitcast(I32), k_scales[0, r:16:4, :].bitcast(I32))
+            queue = nc.scalar if r == 1 else nc.sync
+            queue.dma_start(pool_scales[r:P:32, :].bitcast(I32), k_scales[0, r:16:4, :].bitcast(I32))
         nc.sync.dma_start(pool_words[:, HEAD:], words_in[:, HEAD:])
         for c in range(4):
             load_queries(c, c + 1)

@@ -16,6 +16,7 @@ PACK = 4
 SLOTS, TOKENS, D, NQ = 512, 2048, 512, 512
 HEAD = 768
 QC = 128
+SPLIT = 384
 SHARED = 1
 FLOPS = 2 * SLOTS * D * NQ
 
@@ -33,7 +34,8 @@ def tile_attend_plw_poly_seg_kernel(tc, qT, k_words, k_scales, offs, out_0, out_
         offsets = sb.tile([P, SLOTS // 16], U16, name="offsets")
         pool_scales = sb.tile([P, TOKENS], U8, name="pool_scales", align_bytes=256)
         pool_words = sb.tile([P, TOKENS], I32, name="pool_words", align_bytes=256)
-        nc.vector.memset(pool_scales[:].bitcast(I32), 0)
+        nc.vector.memset(pool_scales[:].bitcast(I32)[:, :SPLIT], 0)
+        nc.gpsimd.memset(pool_scales[:].bitcast(I32)[:, SPLIT:], 0)
         words_in = k_words[0].rearrange("p t r -> p (t r)").bitcast(I32)
         nc.sync.dma_start(pool_words[:, :HEAD], words_in[:, :HEAD])
         nc.sync.dma_start(offsets[:], offs)

@@ -14,9 +14,9 @@ SQUARE = mybir.ActivationFunctionType.Square
 P = 128
 PACK = 4
 SLOTS, TOKENS, D, NQ = 512, 2048, 512, 512
-HEAD = 768
+HEAD = 832
 QC = 128
-SPLIT = 384
+SPLIT = 352
 SHARED = 1
 FLOPS = 2 * SLOTS * D * NQ
 

@@ -14,9 +14,9 @@ SQUARE = mybir.ActivationFunctionType.Square
 P = 128
 PACK = 4
 SLOTS, TOKENS, D, NQ = 512, 2048, 512, 512
-HEAD = 832
+HEAD = 768
 QC = 128
-SPLIT = 352
+SPLIT = 384
 SHARED = 1
 FLOPS = 2 * SLOTS * D * NQ
 
@@ -52,8 +52,9 @@ def tile_attend_plw_poly_seg_kernel(tc, qT, k_words, k_scales, offs, out_0, out_
             queue = nc.scalar if r == 1 else nc.sync
             queue.dma_start(pool_scales[r:P:32, :].bitcast(I32), k_scales[0, r:16:4, :].bitcast(I32))
         nc.sync.dma_start(pool_words[:, HEAD:], words_in[:, HEAD:])
-        for c in range(4):
-            load_queries(c, c + 1)
+        load_queries(0, 2)
+        load_queries(2, 3)
+        load_queries(3, 4)
 
         key_scales = sb.tile([P, SLOTS], U8, name="key_scales", align_bytes=64)
         key_words = sb.tile([P, SLOTS], U32, name="key_words", align_bytes=64)
@@ -75,14 +76,10 @@ def tile_attend_plw_poly_seg_kernel(tc, qT, k_words, k_scales, offs, out_0, out_
                 pool_words[:].bitcast(U32).indirect(offsets[:]),
             )
 
-        def round_queries(c, copy):
-            q_bf[c] = sb.tile([P, QC, PACK], BF16, name="q_bf%d" % c, tag="q_bf%d" % (1 if c == 3 else c), align_bytes=64)
-            interleave(copy, q_bf[c][:], q_raw[c])
-
-        def round_queries_in_halves(c):
-            q_bf[c] = sb.tile([P, QC, PACK], BF16, name="q_bf%d" % c, tag="q_bf0", align_bytes=64)
-            interleave(nc.scalar.copy, q_bf[c][:, : QC // 2, :], q_raw[c][:, :, : QC // 2])
-            interleave(nc.vector.tensor_copy, q_bf[c][:, QC // 2 :, :], q_raw[c][:, :, QC // 2 :])
+        def round_queries(c, copy, first, last):
+            if c not in q_bf:
+                q_bf[c] = sb.tile([P, QC, PACK], BF16, name="q_bf%d" % c, tag="q_bf%d" % (1 if c == 3 else c), align_bytes=64)
+            interleave(copy, q_bf[c][:, first:last, :], q_raw[c][:, :, first:last])
 
         def quantise_queries(c):
             words = sb.tile([P, QC], U32, name="q_words%d" % c, tag="words%d" % c, align_bytes=256)
@@ -154,16 +151,19 @@ def tile_attend_plw_poly_seg_kernel(tc, qT, k_words, k_scales, offs, out_0, out_
         on_scalar, on_vector = nc.scalar.copy, nc.vector.tensor_copy
         gather_scales()
         gather_words()
-        round_queries(0, on_scalar)
+        half = QC // 2
+        round_queries(0, on_scalar, 0, half)
+        round_queries(0, on_vector, half, QC)
+        round_queries(1, on_vector, half, QC)
+        round_queries(1, on_scalar, 0, half)
         quantise_queries(0)
-        round_queries(1, on_scalar)
-        score(0)
         quantise_queries(1)
-        round_queries_in_halves(2)
+        score(0)
+        round_queries(2, on_scalar, 0, QC)
         score(1)
-        weigh(0)
         quantise_queries(2)
-        round_queries(3, on_vector)
+        round_queries(3, on_vector, 0, QC)
+        weigh(0)
         score(2)
         weigh_shared(1)
         shift_on_vector()

@@ -37,8 +37,8 @@ def tile_attend_plw_poly_seg_kernel(tc, qT, k_words, k_scales, offs, out_0, out_
         nc.vector.memset(pool_scales[:].bitcast(I32)[:, :SPLIT], 0)
         nc.gpsimd.memset(pool_scales[:].bitcast(I32)[:, SPLIT:], 0)
         words_in = k_words[0].rearrange("p t r -> p (t r)").bitcast(I32)
-        nc.sync.dma_start(pool_words[:, :HEAD], words_in[:, :HEAD])
         nc.sync.dma_start(offsets[:], offs)
+        nc.sync.dma_start(pool_words[:, :HEAD], words_in[:, :HEAD])
         q_rows = qT[0].rearrange("(p t) q -> p t q", t=PACK)
         q_raw = {}
 
@@ -52,9 +52,8 @@ def tile_attend_plw_poly_seg_kernel(tc, qT, k_words, k_scales, offs, out_0, out_
             queue = nc.scalar if r == 1 else nc.sync
             queue.dma_start(pool_scales[r:P:32, :].bitcast(I32), k_scales[0, r:16:4, :].bitcast(I32))
         nc.sync.dma_start(pool_words[:, HEAD:], words_in[:, HEAD:])
-        load_queries(0, 2)
-        load_queries(2, 3)
-        load_queries(3, 4)
+        for c in range(4):
+            load_queries(c, c + 1)
 
         key_scales = sb.tile([P, SLOTS], U8, name="key_scales", align_bytes=64)
         key_words = sb.tile([P, SLOTS], U32, name="key_words", align_bytes=64)
@@ -76,10 +75,14 @@ def tile_attend_plw_poly_seg_kernel(tc, qT, k_words, k_scales, offs, out_0, out_
                 pool_words[:].bitcast(U32).indirect(offsets[:]),
             )
 
-        def round_queries(c, copy, first, last):
-            if c not in q_bf:
-                q_bf[c] = sb.tile([P, QC, PACK], BF16, name="q_bf%d" % c, tag="q_bf%d" % (1 if c == 3 else c), align_bytes=64)
-            interleave(copy, q_bf[c][:, first:last, :], q_raw[c][:, :, first:last])
+        def round_queries(c, copy):
+            q_bf[c] = sb.tile([P, QC, PACK], BF16, name="q_bf%d" % c, tag="q_bf%d" % (1 if c == 3 else c), align_bytes=64)
+            interleave(copy, q_bf[c][:], q_raw[c])
+
+        def round_queries_in_halves(c):
+            q_bf[c] = sb.tile([P, QC, PACK], BF16, name="q_bf%d" % c, tag="q_bf0", align_bytes=64)
+            interleave(nc.scalar.copy, q_bf[c][:, : QC // 2, :], q_raw[c][:, :, : QC // 2])
+            interleave(nc.vector.tensor_copy, q_bf[c][:, QC // 2 :, :], q_raw[c][:, :, QC // 2 :])
 
         def quantise_queries(c):
             words = sb.tile([P, QC], U32, name="q_words%d" % c, tag="words%d" % c, align_bytes=256)
@@ -151,19 +154,16 @@ def tile_attend_plw_poly_seg_kernel(tc, qT, k_words, k_scales, offs, out_0, out_
         on_scalar, on_vector = nc.scalar.copy, nc.vector.tensor_copy
         gather_scales()
         gather_words()
-        half = QC // 2
-        round_queries(0, on_scalar, 0, half)
-        round_queries(0, on_vector, half, QC)
-        round_queries(1, on_vector, half, QC)
-        round_queries(1, on_scalar, 0, half)
+        round_queries(0, on_scalar)
         quantise_queries(0)
-        quantise_queries(1)
+        round_queries(1, on_scalar)
         score(0)
-        round_queries(2, on_scalar, 0, QC)
+        quantise_queries(1)
+        round_queries_in_halves(2)
         score(1)
-        quantise_queries(2)
-        round_queries(3, on_vector, 0, QC)
         weigh(0)
+        quantise_queries(2)
+        round_queries(3, on_vector)
         score(2)
         weigh_shared(1)
         shift_on_vector()

@@ -37,8 +37,8 @@ def tile_attend_plw_poly_seg_kernel(tc, qT, k_words, k_scales, offs, out_0, out_
         nc.vector.memset(pool_scales[:].bitcast(I32)[:, :SPLIT], 0)
         nc.gpsimd.memset(pool_scales[:].bitcast(I32)[:, SPLIT:], 0)
         words_in = k_words[0].rearrange("p t r -> p (t r)").bitcast(I32)
-        nc.sync.dma_start(offsets[:], offs)
         nc.sync.dma_start(pool_words[:, :HEAD], words_in[:, :HEAD])
+        nc.sync.dma_start(offsets[:], offs)
         q_rows = qT[0].rearrange("(p t) q -> p t q", t=PACK)
         q_raw = {}
 
@@ -97,9 +97,16 @@ def tile_attend_plw_poly_seg_kernel(tc, qT, k_words, k_scales, offs, out_0, out_
             banks[c] = psum.tile([P, PACK, QC], F32, name="bank%d" % c)
             if c == SHARED:
                 banks["side"] = psum.tile([P, QC], F32, name="side_bank")
+            if c == 0:
+                banks["early"] = psum.tile([P, 2, QC], F32, name="early_bank")
             for u in range(PACK):
+                out = banks[c][:, u, :]
+                if (c, u) == (SHARED, 0):
+                    out = banks["side"][:]
+                if c == 0 and u < 2:
+                    out = banks["early"][:, u, :]
                 nc.tensor.matmul_mx(
-                    out=banks["side"][:] if (c, u) == (SHARED, 0) else banks[c][:, u, :],
+                    out=out,
                     lhsT=key_words[:, u * P : (u + 1) * P].bitcast(FP8X4),
                     lhsT_scale=key_scales[:, u * P : (u + 1) * P],
                     rhs=words[:].bitcast(FP8X4),
@@ -112,6 +119,15 @@ def tile_attend_plw_poly_seg_kernel(tc, qT, k_words, k_scales, offs, out_0, out_
             y[c] = sb.tile([P, PACK, QC], F32, name="y%d" % c, align_bytes=256)
             nc.scalar.activation(y[c][:], banks[c][:], SQUARE, bias=1.0)
             nc.sync.dma_start(y_rows[:, :, c * QC : (c + 1) * QC], y[c][:])
+
+        def weigh_first():
+            y[0] = sb.tile([P, PACK, QC], F32, name="y0", align_bytes=256)
+            nc.scalar.activation(y[0][:, :2, :], banks["early"][:], SQUARE, bias=1.0)
+            for u in (0, 1):
+                nc.sync.dma_start(y_rows[:, u, :QC], y[0][:, u, :])
+            nc.scalar.activation(y[0][:, 2:, :], banks[0][:, 2:, :], SQUARE, bias=1.0)
+            for u in (2, 3):
+                nc.sync.dma_start(y_rows[:, u, :QC], y[0][:, u, :])
 
         def shift_on_vector():
             y["shifted"] = sb.tile([P, QC], F32, name="shifted", tag="y_bf0", align_bytes=64)
@@ -161,7 +177,7 @@ def tile_attend_plw_poly_seg_kernel(tc, qT, k_words, k_scales, offs, out_0, out_
         quantise_queries(1)
         round_queries_in_halves(2)
         score(1)
-        weigh(0)
+        weigh_first()
         quantise_queries(2)
         round_queries(3, on_vector)
         score(2)
@@ -177,12 +193,10 @@ def tile_attend_plw_poly_seg_kernel(tc, qT, k_words, k_scales, offs, out_0, out_
         weigh_rounded(3)
         round_weights(2)
         quantise_weights(1)
-        weigh(3)
         store_words(0, 2, nc.sync)
+        weigh(3)
         quantise_weights(2)
         quantise_weights(3)
-        store_words(2, 4, nc.scalar)
-        store_scales(0, nc.sync)
-        store_scales(1, nc.scalar)
-        store_scales(2, nc.sync)
-        store_scales(3, nc.scalar)
+        store_words(2, 4, nc.sync)
+        for quad in range(4):
+            store_scales(quad, nc.sync)

@@ -17,8 +17,9 @@ SLOTS, TOKENS, D, NQ = 512, 2048, 512, 512
 HEAD = 768
 QC = 128
 SPLIT = 384
-SHARED = 1
 FLOPS = 2 * SLOTS * D * NQ
+BANK_PLACES = {0: ((0, 2), (2, 4)), 1: ((0, 2), (2, 4)), 2: ((0, 2), (2, 4)), 3: ((0, 4),)}
+STORE_PLACES = {(0, 0): ((0, 2),), (0, 2): ((2, 4),), (1, 0): ((0, 2),), (1, 2): ((2, 4),), (2, 0): (), (2, 2): ((0, 4),), (3, 0): ((0, 4),)}
 
 
 def interleave(copy, dst, src):
@@ -42,18 +43,13 @@ def tile_attend_plw_poly_seg_kernel(tc, qT, k_words, k_scales, offs, out_0, out_
         q_rows = qT[0].rearrange("(p t) q -> p t q", t=PACK)
         q_raw = {}
 
-        def load_queries(first, last):
-            raw = sb.tile([P, PACK, (last - first) * QC], F32, name="q_raw%d" % first, align_bytes=256)
-            nc.sync.dma_start(raw[:], q_rows[:, :, first * QC : last * QC])
-            for c in range(first, last):
-                q_raw[c] = raw[:, :, (c - first) * QC : (c - first + 1) * QC]
-
         for r in range(4):
             queue = nc.scalar if r == 1 else nc.sync
             queue.dma_start(pool_scales[r:P:32, :].bitcast(I32), k_scales[0, r:16:4, :].bitcast(I32))
         nc.sync.dma_start(pool_words[:, HEAD:], words_in[:, HEAD:])
         for c in range(4):
-            load_queries(c, c + 1)
+            q_raw[c] = sb.tile([P, PACK, QC], F32, name="q_raw%d" % c, align_bytes=256)
+            nc.sync.dma_start(q_raw[c][:], q_rows[:, :, c * QC : (c + 1) * QC])
 
         key_scales = sb.tile([P, SLOTS], U8, name="key_scales", align_bytes=64)
         key_words = sb.tile([P, SLOTS], U32, name="key_words", align_bytes=64)
@@ -77,7 +73,7 @@ def tile_attend_plw_poly_seg_kernel(tc, qT, k_words, k_scales, offs, out_0, out_
 
         def round_queries(c, copy):
             q_bf[c] = sb.tile([P, QC, PACK], BF16, name="q_bf%d" % c, tag="q_bf%d" % (1 if c == 3 else c), align_bytes=64)
-            interleave(copy, q_bf[c][:], q_raw[c])
+            interleave(copy, q_bf[c][:], q_raw[c][:])
 
         def round_queries_in_halves(c):
             q_bf[c] = sb.tile([P, QC, PACK], BF16, name="q_bf%d" % c, tag="q_bf0", align_bytes=64)
@@ -94,60 +90,34 @@ def tile_attend_plw_poly_seg_kernel(tc, qT, k_words, k_scales, offs, out_0, out_
 
         def score(c):
             words, scales = q_mx[c]
-            banks[c] = psum.tile([P, PACK, QC], F32, name="bank%d" % c)
-            if c == SHARED:
-                banks["side"] = psum.tile([P, QC], F32, name="side_bank")
-            if c == 0:
-                banks["early"] = psum.tile([P, 2, QC], F32, name="early_bank")
-            for u in range(PACK):
-                out = banks[c][:, u, :]
-                if (c, u) == (SHARED, 0):
-                    out = banks["side"][:]
-                if c == 0 and u < 2:
-                    out = banks["early"][:, u, :]
-                nc.tensor.matmul_mx(
-                    out=out,
-                    lhsT=key_words[:, u * P : (u + 1) * P].bitcast(FP8X4),
-                    lhsT_scale=key_scales[:, u * P : (u + 1) * P],
-                    rhs=words[:].bitcast(FP8X4),
-                    rhs_scale=scales[:],
-                    start=True,
-                    stop=True,
-                )
+            for first, last in BANK_PLACES[c]:
+                bank = psum.tile([P, last - first, QC], F32, name="bank%d_%d" % (c, first))
+                banks[c, first] = bank
+                for u in range(first, last):
+                    nc.tensor.matmul_mx(
+                        out=bank[:, u - first, :],
+                        lhsT=key_words[:, u * P : (u + 1) * P].bitcast(FP8X4),
+                        lhsT_scale=key_scales[:, u * P : (u + 1) * P],
+                        rhs=words[:].bitcast(FP8X4),
+                        rhs_scale=scales[:],
+                        start=True,
+                        stop=True,
+                    )
 
         def weigh(c):
             y[c] = sb.tile([P, PACK, QC], F32, name="y%d" % c, align_bytes=256)
-            nc.scalar.activation(y[c][:], banks[c][:], SQUARE, bias=1.0)
-            nc.sync.dma_start(y_rows[:, :, c * QC : (c + 1) * QC], y[c][:])
-
-        def weigh_first():
-            y[0] = sb.tile([P, PACK, QC], F32, name="y0", align_bytes=256)
-            nc.scalar.activation(y[0][:, :2, :], banks["early"][:], SQUARE, bias=1.0)
-            for u in (0, 1):
-                nc.sync.dma_start(y_rows[:, u, :QC], y[0][:, u, :])
-            nc.scalar.activation(y[0][:, 2:, :], banks[0][:, 2:, :], SQUARE, bias=1.0)
-            for u in (2, 3):
-                nc.sync.dma_start(y_rows[:, u, :QC], y[0][:, u, :])
-
-        def shift_on_vector():
-            y["shifted"] = sb.tile([P, QC], F32, name="shifted", tag="y_bf0", align_bytes=64)
-            nc.vector.tensor_scalar_add(y["shifted"][:], banks["side"][:], 1.0)
-
-        def weigh_shared(c):
-            y[c] = sb.tile([P, PACK, QC], F32, name="y%d" % c, align_bytes=256)
-            nc.scalar.activation(y[c][:, 1:, :], banks[c][:, 1:, :], SQUARE, bias=1.0)
-
-        def square_on_vector(c):
-            nc.vector.tensor_mul(y[c][:, 0, :], y["shifted"][:], y["shifted"][:])
-            nc.sync.dma_start(y_rows[:, :, c * QC : (c + 1) * QC], y[c][:])
+            for first, last in BANK_PLACES[c]:
+                nc.scalar.activation(y[c][:, first:last, :], banks[c, first][:], SQUARE, bias=1.0)
+                for a, b in STORE_PLACES[c, first]:
+                    nc.sync.dma_start(y_rows[:, a:b, c * QC : (c + 1) * QC], y[c][:, a:b, :])
 
         def round_weights(c):
-            y_bf[c] = sb.tile([P, QC, PACK], BF16, name="y_bf%d" % c, align_bytes=64)
+            y_bf[c] = sb.tile([P, QC, PACK], BF16, name="y_bf%d" % c, tag="q_bf1" if c == 0 else "y_bf%d" % c, align_bytes=64)
             interleave(nc.vector.tensor_copy, y_bf[c][:], y[c][:])
 
         def weigh_rounded(c):
             y_bf[c] = sb.tile([P, QC, PACK], BF16, name="y_bf%d" % c, align_bytes=64)
-            nc.scalar.activation(y_bf[c][:], banks[c][:].rearrange("p u q -> p q u"), SQUARE, bias=1.0)
+            nc.scalar.activation(y_bf[c][:], banks[c, 0][:].rearrange("p u q -> p q u"), SQUARE, bias=1.0)
 
         def quantise_weights(c):
             cols = slice(c * QC, (c + 1) * QC)
@@ -157,11 +127,12 @@ def tile_attend_plw_poly_seg_kernel(tc, qT, k_words, k_scales, offs, out_0, out_
                 in_=y_bf[c][:].rearrange("p q u -> p (q u)"),
             )
 
-        def store_words(first, last, queue):
+        def store_words(first, last):
             cols = slice(first * QC, last * QC)
-            queue.dma_start(words_out[:, cols], y_words[:, cols])
+            nc.sync.dma_start(words_out[:, cols], y_words[:, cols])
 
-        def store_scales(quad, queue):
+        def store_scales(quad):
+            queue = nc.scalar if quad % 2 else nc.sync
             queue.dma_start(
                 out_2[0, 4 * quad : 4 * quad + 4, :].bitcast(I32),
                 y_scales[32 * quad : 32 * quad + 4, :].bitcast(I32),
@@ -177,15 +148,13 @@ def tile_attend_plw_poly_seg_kernel(tc, qT, k_words, k_scales, offs, out_0, out_
         quantise_queries(1)
         round_queries_in_halves(2)
         score(1)
-        weigh_first()
+        weigh(0)
         quantise_queries(2)
         round_queries(3, on_vector)
         score(2)
-        weigh_shared(1)
-        shift_on_vector()
+        weigh(1)
         quantise_queries(3)
         score(3)
-        square_on_vector(1)
         round_weights(0)
         weigh(2)
         round_weights(1)
@@ -193,10 +162,10 @@ def tile_attend_plw_poly_seg_kernel(tc, qT, k_words, k_scales, offs, out_0, out_
         weigh_rounded(3)
         round_weights(2)
         quantise_weights(1)
-        store_words(0, 2, nc.sync)
+        store_words(0, 2)
         weigh(3)
         quantise_weights(2)
         quantise_weights(3)
-        store_words(2, 4, nc.sync)
+        store_words(2, 4)
         for quad in range(4):
-            store_scales(quad, nc.sync)
+            store_scales(quad)

@@ -19,11 +19,11 @@ QC = 128
 SPLIT = 384
 FLOPS = 2 * SLOTS * D * NQ
 BANK_PLACES = {0: ((0, 2), (2, 4)), 1: ((0, 2), (2, 4)), 2: ((0, 2), (2, 4)), 3: ((0, 4),)}
-STORE_PLACES = {(0, 0): ((0, 2),), (0, 2): ((2, 4),), (1, 0): ((0, 2),), (1, 2): ((2, 4),), (2, 0): (), (2, 2): ((0, 4),), (3, 0): ((0, 4),)}
+STORE_PLACES = {(0, 0): ((0, 1), (1, 2)), (0, 2): ((2, 4),), (1, 0): ((0, 2),), (1, 2): ((2, 4),), (2, 0): (), (2, 2): ((0, 4),), (3, 0): ((0, 4),)}
 
 
 def interleave(copy, dst, src):
-    copy(dst.rearrange("p (c i) t -> p c t i", i=4), src.rearrange("p t (c i) -> p c t i", i=4))
+    copy(dst.rearrange("p (c i) t -> p c t i", i=2), src.rearrange("p t (c i) -> p c t i", i=2))
 
 
 def tile_attend_plw_poly_seg_kernel(tc, qT, k_words, k_scales, offs, out_0, out_1, out_2):
@@ -132,8 +132,7 @@ def tile_attend_plw_poly_seg_kernel(tc, qT, k_words, k_scales, offs, out_0, out_
             nc.sync.dma_start(words_out[:, cols], y_words[:, cols])
 
         def store_scales(quad):
-            queue = nc.scalar if quad % 2 else nc.sync
-            queue.dma_start(
+            nc.sync.dma_start(
                 out_2[0, 4 * quad : 4 * quad + 4, :].bitcast(I32),
                 y_scales[32 * quad : 32 * quad + 4, :].bitcast(I32),
             )

@@ -17,9 +17,10 @@ SLOTS, TOKENS, D, NQ = 512, 2048, 512, 512
 HEAD = 768
 QC = 128
 SPLIT = 384
+SHARE = 48
 FLOPS = 2 * SLOTS * D * NQ
-BANK_PLACES = {0: ((0, 2), (2, 4)), 1: ((0, 2), (2, 4)), 2: ((0, 2), (2, 4)), 3: ((0, 4),)}
-STORE_PLACES = {(0, 0): ((0, 1), (1, 2)), (0, 2): ((2, 4),), (1, 0): ((0, 2),), (1, 2): ((2, 4),), (2, 0): (), (2, 2): ((0, 4),), (3, 0): ((0, 4),)}
+BANK_PLACES = {0: ((0, 2), (2, 4)), 1: ((0, 2), (2, 4)), 2: ((0, 2), (2, 4)), 3: ((0, 2), (2, 4))}
+STORE_PLACES = {(0, 0): ((0, 1), (1, 2)), (0, 2): ((2, 4),), (1, 0): ((0, 2),), (1, 2): ((2, 4),), (2, 0): (), (2, 2): ((0, 4),), (3, 0): (), (3, 2): ((0, 4),)}
 
 
 def interleave(copy, dst, src):
@@ -115,9 +116,10 @@ def tile_attend_plw_poly_seg_kernel(tc, qT, k_words, k_scales, offs, out_0, out_
             y_bf[c] = sb.tile([P, QC, PACK], BF16, name="y_bf%d" % c, tag="q_bf1" if c == 0 else "y_bf%d" % c, align_bytes=64)
             interleave(nc.vector.tensor_copy, y_bf[c][:], y[c][:])
 
-        def weigh_rounded(c):
+        def round_weights_shared(c):
             y_bf[c] = sb.tile([P, QC, PACK], BF16, name="y_bf%d" % c, align_bytes=64)
-            nc.scalar.activation(y_bf[c][:], banks[c, 0][:].rearrange("p u q -> p q u"), SQUARE, bias=1.0)
+            interleave(nc.scalar.copy, y_bf[c][:, : SHARE, :], y[c][:, :, : SHARE])
+            interleave(nc.vector.tensor_copy, y_bf[c][:, SHARE :, :], y[c][:, :, SHARE :])
 
         def quantise_weights(c):
             cols = slice(c * QC, (c + 1) * QC)
@@ -158,11 +160,11 @@ def tile_attend_plw_poly_seg_kernel(tc, qT, k_words, k_scales, offs, out_0, out_
         weigh(2)
         round_weights(1)
         quantise_weights(0)
-        weigh_rounded(3)
+        weigh(3)
         round_weights(2)
         quantise_weights(1)
         store_words(0, 2)
-        weigh(3)
+        round_weights_shared(3)
         quantise_weights(2)
         quantise_weights(3)
         store_words(2, 4)

from contextlib import ExitStack

import concourse.mybir as mybir

F32 = mybir.dt.float32
BF16 = mybir.dt.bfloat16
I32 = mybir.dt.int32
U32 = mybir.dt.uint32
U16 = mybir.dt.uint16
U8 = mybir.dt.uint8
FP8X4 = mybir.dt.float8_e4m3fn_x4
SQUARE = mybir.ActivationFunctionType.Square

P = 128
PACK = 4
SLOTS, TOKENS, D, NQ = 512, 2048, 512, 512
HEAD = 768
QC = 128
SPLIT = 384
SHARE = 48
FLOPS = 2 * SLOTS * D * NQ
BANK_PLACES = {0: ((0, 2), (2, 4)), 1: ((0, 2), (2, 4)), 2: ((0, 2), (2, 4)), 3: ((0, 2), (2, 4))}
STORE_PLACES = {(0, 0): ((0, 1), (1, 2)), (0, 2): ((2, 4),), (1, 0): ((0, 2),), (1, 2): ((2, 4),), (2, 0): (), (2, 2): ((0, 4),), (3, 0): (), (3, 2): ((0, 4),)}


def interleave(copy, dst, src):
    copy(dst.rearrange("p (c i) t -> p c t i", i=2), src.rearrange("p t (c i) -> p c t i", i=2))


def tile_attend_plw_poly_seg_kernel(tc, qT, k_words, k_scales, offs, out_0, out_1, out_2):
    nc = tc.nc
    with ExitStack() as ctx:
        sb = ctx.enter_context(tc.tile_pool(name="sb", bufs=1))
        psum = ctx.enter_context(tc.psum_pool(name="psum", bufs=1))

        offsets = sb.tile([P, SLOTS // 16], U16, name="offsets")
        pool_scales = sb.tile([P, TOKENS], U8, name="pool_scales", align_bytes=256)
        pool_words = sb.tile([P, TOKENS], I32, name="pool_words", align_bytes=256)
        nc.vector.memset(pool_scales[:].bitcast(I32)[:, :SPLIT], 0)
        nc.gpsimd.memset(pool_scales[:].bitcast(I32)[:, SPLIT:], 0)
        words_in = k_words[0].rearrange("p t r -> p (t r)").bitcast(I32)
        nc.sync.dma_start(pool_words[:, :HEAD], words_in[:, :HEAD])
        nc.sync.dma_start(offsets[:], offs)
        q_rows = qT[0].rearrange("(p t) q -> p t q", t=PACK)
        q_raw = {}

        for r in range(4):
            queue = nc.scalar if r == 1 else nc.sync
            queue.dma_start(pool_scales[r:P:32, :].bitcast(I32), k_scales[0, r:16:4, :].bitcast(I32))
        nc.sync.dma_start(pool_words[:, HEAD:], words_in[:, HEAD:])
        for c in range(4):
            q_raw[c] = sb.tile([P, PACK, QC], F32, name="q_raw%d" % c, align_bytes=256)
            nc.sync.dma_start(q_raw[c][:], q_rows[:, :, c * QC : (c + 1) * QC])

        key_scales = sb.tile([P, SLOTS], U8, name="key_scales", align_bytes=64)
        key_words = sb.tile([P, SLOTS], U32, name="key_words", align_bytes=64)
        y_words = sb.tile([P, NQ], I32, name="y_words", align_bytes=256)
        y_scales = sb.tile([P, NQ], U8, name="y_scales", align_bytes=256)
        y_rows = out_0.rearrange("(p u) q -> p u q", u=PACK)
        words_out = out_1[0].rearrange("p q u -> p (q u)").bitcast(I32)
        q_bf, q_mx, banks, y, y_bf = {}, {}, {}, {}, {}

        def gather_scales():
            nc.vector.tensor_copy(
                key_scales[:].rearrange("p (u s) -> p s u", u=PACK),
                pool_scales[:].indirect(offsets[:]),
            )

        def gather_words():
            nc.vector.tensor_copy(
                key_words[:].rearrange("p (u s) -> p s u", u=PACK),
                pool_words[:].bitcast(U32).indirect(offsets[:]),
            )

        def round_queries(c, copy):
            q_bf[c] = sb.tile([P, QC, PACK], BF16, name="q_bf%d" % c, tag="q_bf%d" % (1 if c == 3 else c), align_bytes=64)
            interleave(copy, q_bf[c][:], q_raw[c][:])

        def round_queries_in_halves(c):
            q_bf[c] = sb.tile([P, QC, PACK], BF16, name="q_bf%d" % c, tag="q_bf0", align_bytes=64)
            interleave(nc.scalar.copy, q_bf[c][:, : QC // 2, :], q_raw[c][:, :, : QC // 2])
            interleave(nc.vector.tensor_copy, q_bf[c][:, QC // 2 :, :], q_raw[c][:, :, QC // 2 :])

        def quantise_queries(c):
            words = sb.tile([P, QC], U32, name="q_words%d" % c, tag="words%d" % c, align_bytes=256)
            scales = sb.tile([P, QC], U8, name="q_scales%d" % c, align_bytes=64)
            nc.vector.quantize_mx(
                out=words[:].bitcast(FP8X4), scales=scales[:], in_=q_bf[c][:].rearrange("p q t -> p (q t)")
            )
            q_mx[c] = (words, scales)

        def score(c):
            words, scales = q_mx[c]
            for first, last in BANK_PLACES[c]:
                bank = psum.tile([P, last - first, QC], F32, name="bank%d_%d" % (c, first))
                banks[c, first] = bank
                for u in range(first, last):
                    nc.tensor.matmul_mx(
                        out=bank[:, u - first, :],
                        lhsT=key_words[:, u * P : (u + 1) * P].bitcast(FP8X4),
                        lhsT_scale=key_scales[:, u * P : (u + 1) * P],
                        rhs=words[:].bitcast(FP8X4),
                        rhs_scale=scales[:],
                        start=True,
                        stop=True,
                    )

        def weigh(c):
            y[c] = sb.tile([P, PACK, QC], F32, name="y%d" % c, align_bytes=256)
            for first, last in BANK_PLACES[c]:
                nc.scalar.activation(y[c][:, first:last, :], banks[c, first][:], SQUARE, bias=1.0)
                for a, b in STORE_PLACES[c, first]:
                    nc.sync.dma_start(y_rows[:, a:b, c * QC : (c + 1) * QC], y[c][:, a:b, :])

        def round_weights(c):
            y_bf[c] = sb.tile([P, QC, PACK], BF16, name="y_bf%d" % c, tag="q_bf1" if c == 0 else "y_bf%d" % c, align_bytes=64)
            interleave(nc.vector.tensor_copy, y_bf[c][:], y[c][:])

        def round_weights_shared(c):
            y_bf[c] = sb.tile([P, QC, PACK], BF16, name="y_bf%d" % c, align_bytes=64)
            interleave(nc.scalar.copy, y_bf[c][:, : SHARE, :], y[c][:, :, : SHARE])
            interleave(nc.vector.tensor_copy, y_bf[c][:, SHARE :, :], y[c][:, :, SHARE :])

        def quantise_weights(c):
            cols = slice(c * QC, (c + 1) * QC)
            nc.vector.quantize_mx(
                out=y_words[:, cols].bitcast(FP8X4),
                scales=y_scales[:, cols],
                in_=y_bf[c][:].rearrange("p q u -> p (q u)"),
            )

        def store_words(first, last):
            cols = slice(first * QC, last * QC)
            nc.sync.dma_start(words_out[:, cols], y_words[:, cols])

        def store_scales(quad):
            nc.sync.dma_start(
                out_2[0, 4 * quad : 4 * quad + 4, :].bitcast(I32),
                y_scales[32 * quad : 32 * quad + 4, :].bitcast(I32),
            )

        on_scalar, on_vector = nc.scalar.copy, nc.vector.tensor_copy
        gather_scales()
        gather_words()
        round_queries(0, on_scalar)
        quantise_queries(0)
        round_queries(1, on_scalar)
        score(0)
        quantise_queries(1)
        round_queries_in_halves(2)
        score(1)
        weigh(0)
        quantise_queries(2)
        round_queries(3, on_vector)
        score(2)
        weigh(1)
        quantise_queries(3)
        score(3)
        round_weights(0)
        weigh(2)
        round_weights(1)
        quantise_weights(0)
        weigh(3)
        round_weights(2)
        quantise_weights(1)
        store_words(0, 2)
        round_weights_shared(3)
        quantise_weights(2)
        quantise_weights(3)
        store_words(2, 4)
        for quad in range(4):
            store_scales(quad)
